import numpy as np
import ml_dtypes


def mxq(x, axis, fmt="e4m3"):
    dtype, down = {"e4m3": (ml_dtypes.float8_e4m3fn, 7), "e5m2": (ml_dtypes.float8_e5m2, 14)}[fmt]
    v = np.moveaxis(np.asarray(x, np.float32).astype(ml_dtypes.bfloat16).astype(np.float64), axis, -1)
    blocks = v.reshape(v.shape[:-1] + (-1, 32))
    amax = np.abs(blocks).max(-1, keepdims=True)
    byte = np.maximum(np.where(amax > 0, np.frexp(amax)[1] - 1 + 127, 0) - down, 1)
    scale = np.exp2(byte - 127.0)
    codes = (blocks / scale).astype(np.float32).astype(dtype).astype(np.float64)
    return np.moveaxis((codes * scale).reshape(v.shape), -1, axis)


WIDE = False


def mx_kscale(k):
    if not WIDE:
        return np.ones(k)
    levels = np.array([24, -24, 12, -12, 0])
    if k % 512:
        return np.exp2(np.random.permutation(np.resize(levels, k // 32))).repeat(32)
    a = np.empty((k // 512, 16))
    for p in range(k // 512):
        a[p, :8] = np.random.permutation(np.resize(levels, 8))
        for g in range(8):
            far = levels[np.abs(levels - a[p, g]) >= 10]
            a[p, g + 8] = far[np.random.randint(len(far))]
    return np.exp2(a.ravel()).repeat(32)


def f64(x):
    return np.asarray(x).astype(np.float64)


def striped(idx):
    return np.tile(idx.reshape(-1, 16).T, (8, 1)).astype(np.uint16)


def unstriped(offs):
    return offs[:16].T.reshape(-1).astype(np.int64)


E2M1 = np.array([0.0, 0.5, 1.0, 1.5, 2.0, 3.0, 4.0, 6.0, -0.0, -0.5, -1.0, -1.5, -2.0, -3.0, -4.0, -6.0])


def pack_weight(w, fmt):
    k, n = w.shape
    w = f64(np.asarray(w, np.float32).astype(ml_dtypes.bfloat16)).reshape(k // 32, 32, n)
    amax = np.abs(w).max(1)
    if fmt == "e4m3":
        byte = np.frexp(amax)[1] - 1 + 127 - 7
    else:
        mant, ex = np.frexp(amax / 6.0)
        byte = np.where(mant > 0.5, ex, ex - 1) + 127
    byte = np.clip(np.where(amax > 0, byte, 1), 1, 254)
    scaled = (w * np.exp2(127.0 - byte)[:, None, :]).reshape(k, n).astype(np.float32)
    by_word = np.ascontiguousarray(scaled.reshape(k // 512, 128, 4, n).transpose(0, 1, 3, 2))
    if fmt == "e4m3":
        words = by_word.astype(ml_dtypes.float8_e4m3fn).view(np.uint8)
    else:
        c = by_word.astype(ml_dtypes.float4_e2m1fn).view(np.uint8) & 0xF
        words = (c[..., 0::2] | (c[..., 1::2] << 4)).reshape(k // 512, 128, 2 * n)
    return np.ascontiguousarray(words), np.ascontiguousarray(byte.astype(np.uint8).reshape(k // 512, 16, n))


def unpack_weight(words, scales, fmt):
    g, _, n = scales.shape
    words = np.ascontiguousarray(words).reshape(g, 128, n, -1)
    if fmt == "e4m3":
        vals = words.view(ml_dtypes.float8_e4m3fn).astype(np.float64)
    else:
        nib = np.empty((g, 128, n, 4), np.uint8)
        nib[..., 0::2] = words & 0xF
        nib[..., 1::2] = words >> 4
        vals = E2M1[nib]
    vals = vals * np.repeat(np.exp2(scales.astype(np.float64) - 127.0), 8, axis=1)[..., None]
    return vals.transpose(0, 1, 3, 2).reshape(g * 512, n)


def pack_table4(v):
    words, scales = pack_weight(v, "e2m1")
    g, t = words.shape[0] // 2, v.shape[1]
    return np.ascontiguousarray(words.reshape(g, 2, 128, t, 2).transpose(0, 2, 3, 1, 4).reshape(g, 128, t, 4)), scales


def unpack_table4(words, scales):
    g, _, t, _ = words.shape
    return unpack_weight(words.reshape(g, 128, t, 2, 2).transpose(0, 3, 1, 2, 4).reshape(2 * g, 128, 2 * t), scales, "e2m1")


K, R, N, T, J = 1024, 1024, 1024, 1024, 512


def setup_inputs():
    n = np.random.standard_normal
    s = mx_kscale(K)[:, None]
    u = mx_kscale(R)[:, None]
    p_tab = pack_table4(n((K, T)) * s)
    p_wb = pack_weight(0.7 * n((K, N)) / np.sqrt(K) / s, "e4m3")
    p_dn = pack_weight(n((K, R)) / np.sqrt(K) / s * u.T, "e4m3")
    return {
        "tab_words": p_tab[0],
        "tab_scales": p_tab[1],
        "wb_words": p_wb[0],
        "wb_scales": p_wb[1],
        "dn_words": p_dn[0],
        "dn_scales": p_dn[1],
        "upw": (2.0 * n((R, N)) / np.sqrt(R) / u).astype(np.float32),
        "x0T": (n((N, T))).astype(np.float32),
        "b": (0.3 * n(N)).astype(np.float32),
        "offs": striped(np.random.permutation(T)[:J]),
    }


def reference(tab_words, tab_scales, wb_words, wb_scales, dn_words, dn_scales, upw, x0T, b, offs):
    idx = unstriped(offs)
    tab_ = unpack_table4(tab_words, tab_scales)[:, idx]
    wb_ = unpack_weight(wb_words, wb_scales, "e4m3")
    dn_ = unpack_weight(dn_words, dn_scales, "e4m3")
    hs = dn_.T @ tab_
    h = hs
    h_ = mxq(h, 0, "e4m3")
    upw_ = mxq(f64(upw), 0, "e4m3")
    y = wb_.T @ tab_ + upw_.T @ h_
    return f64(x0T)[:, idx] * (y + f64(b)[:, None]) + f64(x0T)[:, idx]

@@ -1,0 +1,248 @@
+from contextlib import ExitStack
+
+import concourse.mybir as mybir
+from concourse.masks import make_identity
+
+K, R, N, T, J = 1024, 1024, 1024, 1024, 512
+FLOPS = 2 * J * (K * R + K * N + R * N)
+
+F32 = mybir.dt.float32
+BF16 = mybir.dt.bfloat16
+I32 = mybir.dt.int32
+U32 = mybir.dt.uint32
+U16 = mybir.dt.uint16
+U8 = mybir.dt.uint8
+FP8X4 = mybir.dt.float8_e4m3fn_x4
+FP4X4 = mybir.dt.float4_e2m1fn_x4
+ACT = mybir.ActivationFunctionType
+ALU = mybir.AluOpType
+
+P = 128
+PACK = 4
+PASS = P * PACK
+PASSES = K // PASS
+NT = N // P
+JC = 128
+HALF = 512
+
+
+def tile_list_xcross_none_kernel(
+    tc, tab_words, tab_scales, wb_words, wb_scales, dn_words, dn_scales, upw, x0T, b, offs, out
+):
+    nc = tc.nc
+    with ExitStack() as ctx:
+        keep = ctx.enter_context(tc.tile_pool(name="keep", bufs=1))
+        ring = ctx.enter_context(tc.tile_pool(name="ring", bufs=3))
+        psum_h = ctx.enter_context(tc.psum_pool(name="psum_h", bufs=3))
+        psum_y = ctx.enter_context(tc.psum_pool(name="psum_y", bufs=5))
+
+        def held(name, shape, dtype):
+            return keep.tile(shape, dtype, name=name, align_bytes=64)
+
+        def load_scales(plane, scales, quadrants):
+            rows = scales.bitcast(I32)
+            for q in quadrants:
+                nc.sync.dma_start(
+                    out=plane[32 * q : 32 * q + 4, :].rearrange("p (a w) -> p a w", a=PASSES),
+                    in_=rows[:, 4 * q : 4 * q + 4, :].rearrange("a r w -> r a w"),
+                )
+
+        def load_words(name, words):
+            tile = held(name, [P, PASSES, words.shape[2]], I32)
+            nc.sync.dma_start(out=tile[:], in_=words.rearrange("a p n i -> p a (n i)").bitcast(I32))
+            return tile
+
+        offsets = keep.tile([P, J // 16], U16, name="offsets")
+        tab_plane = held("tab_plane", [P, PASSES * T // 4], I32)
+        dn_plane = held("dn_plane", [P, PASSES * R // 4], I32)
+        wb_plane = held("wb_plane", [P, PASSES * N // 4], I32)
+        nc.gpsimd.memset(tab_plane[:], 0)
+        nc.vector.memset(dn_plane[:], 0)
+        nc.vector.memset(wb_plane[:], 0)
+        b_rows = held("b_rows", [P, P], F32)
+        nc.gpsimd.memset(b_rows[:], 0.0)
+        ident = held("ident", [P, P], F32)
+        make_identity(nc, ident[:])
+
+        up_raw = {}
+
+        def load_up(a, nh):
+            raw = held("up_raw%d%d" % (a, nh), [P, PACK, HALF], F32)
+            rows = upw[a * PASS : (a + 1) * PASS, nh * HALF : (nh + 1) * HALF]
+            nc.sync.dma_start(out=raw[:], in_=rows.rearrange("(p t) n -> p t n", t=PACK))
+            up_raw[a, nh] = raw
+
+        x0 = {}
+
+        def load_x0(c):
+            tile = held("x0_%d" % c, [P, T], F32)
+            nc.sync.dma_start(out=tile[:], in_=x0T[c * P : (c + 1) * P, :])
+            x0[c] = tile
+
+        nc.sync.dma_start(offsets[:], offs)
+        tab_raw = held("tab_raw", [P, T], I32)
+        dn_raw = {}
+
+        def load_dn(g):
+            tile = held("dn_raw%d" % g, [P, PASSES, PASS], I32)
+            words = dn_words.rearrange("a p n i -> p a (n i)").bitcast(I32)
+            nc.sync.dma_start(out=tile[:], in_=words[:, :, g * PASS : (g + 1) * PASS])
+            dn_raw[g] = tile
+
+        nc.sync.dma_start(out=tab_raw[:], in_=tab_words[0].rearrange("p t i -> p (t i)").bitcast(I32))
+        load_scales(tab_plane, tab_scales, (0, 1, 2, 3))
+        load_dn(0)
+        load_scales(dn_plane, dn_scales, (0, 1))
+        load_up(0, 0)
+        load_scales(dn_plane, dn_scales, (2, 3))
+        load_dn(1)
+        load_up(1, 0)
+        load_up(0, 1)
+        load_scales(wb_plane, wb_scales, (0, 1, 2, 3))
+        nc.sync.dma_start(out=b_rows[0:NT, :], in_=b.rearrange("(c p) -> c p", p=P))
+        wb_codes = load_words("wb_codes", wb_words)
+        load_x0(0)
+        load_x0(1)
+        load_up(1, 1)
+        for c in range(2, NT):
+            load_x0(c)
+
+        tab_pairs = held("tab_pairs", [P, J], U32)
+        tab_codes = held("tab_codes", [P, PASSES, 2 * J], U8)
+        tab_sc = held("tab_sc", [P, PASSES, J], U8)
+        dn_codes = [held("dn_codes%d" % g, [P, PASSES, PASS], I32) for g in range(R // PASS)]
+        dn_sc = [held("dn_sc%d" % g, [P, PASSES, PASS], U8) for g in range(R // PASS)]
+        dn_sc_raw = dn_plane[:].bitcast(U8).rearrange("p (a r) -> p a r", a=PASSES)
+
+        nc.vector.tensor_copy(tab_pairs[:], tab_raw[:].bitcast(U32).indirect(offsets[:]))
+        nc.vector.tensor_copy(tab_sc[:, 0, :], tab_plane[:].bitcast(U8)[:, 0:T].indirect(offsets[:]))
+        nc.vector.tensor_copy(
+            out=tab_codes[:].bitcast(U16),
+            in_=tab_pairs[:].bitcast(U16).rearrange("p (j a) -> p a j", a=PASSES),
+        )
+        nc.vector.tensor_copy(tab_sc[:, 1, :], tab_plane[:].bitcast(U8)[:, T : 2 * T].indirect(offsets[:]))
+
+        def permute_dn(g):
+            cols = slice(g * PASS, (g + 1) * PASS)
+            nc.vector.tensor_copy(
+                out=dn_codes[g][:].rearrange("p a (t m) -> p a m t", t=PACK),
+                in_=dn_raw[g][:].rearrange("p a (m t) -> p a m t", t=PACK),
+            )
+            nc.vector.tensor_copy(
+                out=dn_sc[g][:].rearrange("p a (t m) -> p a m t", t=PACK),
+                in_=dn_sc_raw[:, :, cols].rearrange("p a (m t) -> p a m t", t=PACK),
+            )
+
+        permute_dn(0)
+        permute_dn(1)
+        wb_sc = wb_plane[:].bitcast(U8).rearrange("p (a n) -> p a n", a=PASSES)
+
+        b_ps = psum_y.tile([P, P], F32, name="y_ps")
+        nc.tensor.transpose(b_ps[:], b_rows[:], ident[:])
+        bias1 = held("bias1", [P, NT], F32)
+        nc.scalar.activation(out=bias1[:], in_=b_ps[:, 0:NT], func=ACT.Copy, bias=1.0)
+
+        up_codes = held("up_codes", [P, PASSES, N], U32)
+        up_sc = held("up_sc", [P, PASSES, N], U8)
+        up_bf = {}
+
+        def round_up(a, nh, on_vector, parts):
+            grouped = held("up_bf%d%d" % (a, nh), [P, HALF, PACK], BF16)
+            up_bf[a, nh] = grouped
+            width = HALF // parts
+            for s in range(parts):
+                cols = slice(s * width, (s + 1) * width)
+                dst = grouped[:, cols, :].rearrange("p (c i) t -> p c t i", i=4)
+                src = up_raw[a, nh][:, :, cols].rearrange("p t (c i) -> p c t i", i=4)
+                if on_vector:
+                    nc.vector.tensor_copy(out=dst, in_=src)
+                else:
+                    nc.scalar.copy(out=dst, in_=src)
+
+        def quant_up(a, nh, parts):
+            width = HALF // parts
+            for s in range(parts):
+                cols = slice(nh * HALF + s * width, nh * HALF + (s + 1) * width)
+                nc.vector.quantize_mx(
+                    out=up_codes[:, a, cols].bitcast(FP8X4),
+                    scales=up_sc[:, a, cols],
+                    in_=up_bf[a, nh][:, s * width : (s + 1) * width, :].rearrange("p n t -> p (n t)"),
+                )
+
+        h_codes = held("h_codes", [P, PASSES, J], U32)
+        h_sc = held("h_sc", [P, PASSES, J], U8)
+        h_bf = {}
+
+        def make_h(g):
+            grouped = held("h_bf%d" % g, [P, J, PACK], BF16)
+            h_bf[g] = grouped
+            for jc in range(J // JC):
+                bank = psum_h.tile([P, PACK, JC], F32, name="h_ps")
+                for t in range(PACK):
+                    cols = slice(t * P, (t + 1) * P)
+                    for a in range(PASSES):
+                        nc.tensor.matmul_mx(
+                            out=bank[:, t, :],
+                            lhsT=dn_codes[g][:, a, cols].bitcast(FP8X4),
+                            lhsT_scale=dn_sc[g][:, a, cols],
+                            rhs=tab_codes[:, a, 2 * jc * JC : 2 * (jc + 1) * JC].bitcast(FP4X4),
+                            rhs_scale=tab_sc[:, a, jc * JC : (jc + 1) * JC],
+                            start=(a == 0),
+                            stop=(a == PASSES - 1),
+                        )
+                nc.scalar.copy(
+                    out=grouped[:, jc * JC : (jc + 1) * JC, :], in_=bank[:].rearrange("p t j -> p j t")
+                )
+
+        def quant_h(g):
+            nc.vector.quantize_mx(
+                out=h_codes[:, g, :].bitcast(FP8X4),
+                scales=h_sc[:, g, :],
+                in_=h_bf[g][:].rearrange("p j t -> p (j t)"),
+            )
+
+        def make_out(c):
+            cols = slice(c * P, (c + 1) * P)
+            acc = psum_y.tile([P, J], F32, name="y_ps")
+            for a in range(PASSES):
+                nc.tensor.matmul_mx(
+                    out=acc[:],
+                    lhsT=wb_codes[:, a, cols].bitcast(FP8X4),
+                    lhsT_scale=wb_sc[:, a, cols],
+                    rhs=tab_codes[:, a, :].bitcast(FP4X4),
+                    rhs_scale=tab_sc[:, a, :],
+                    start=(a == 0),
+                    stop=False,
+                )
+            for g in range(PASSES):
+                nc.tensor.matmul_mx(
+                    out=acc[:],
+                    lhsT=up_codes[:, g, cols].bitcast(FP8X4),
+                    lhsT_scale=up_sc[:, g, cols],
+                    rhs=h_codes[:, g, :].bitcast(FP8X4),
+                    rhs_scale=h_sc[:, g, :],
+                    start=False,
+                    stop=(g == PASSES - 1),
+                )
+            factor = ring.tile([P, J], F32, name="factor")
+            nc.scalar.activation(out=factor[:], in_=acc[:], func=ACT.Identity, bias=bias1[:, c : c + 1])
+            result = held("result%d" % c, [P, J], F32)
+            nc.vector.tensor_tensor(result[:], x0[c][:].indirect(offsets[:]), factor[:], ALU.mult)
+            nc.sync.dma_start(out=out[cols, :], in_=result[:])
+
+        make_h(0)
+        make_h(1)
+        round_up(0, 0, False, 4)
+        round_up(1, 0, True, 1)
+        quant_up(0, 0, 1)
+        quant_up(1, 0, 1)
+        quant_h(0)
+        round_up(0, 1, True, 1)
+        quant_h(1)
+        quant_up(0, 1, 1)
+        for c in range(NT // 2):
+            make_out(c)
+        round_up(1, 1, False, 4)
+        quant_up(1, 1, 2)
+        for c in range(NT // 2, NT):
+            make_out(c)

@@ -22,7 +22,6 @@ PACK = 4
 PASS = P * PACK
 PASSES = K // PASS
 NT = N // P
-JC = 128
 HALF = 512
 
 
@@ -32,25 +31,29 @@ def tile_list_xcross_none_kernel(
     nc = tc.nc
     with ExitStack() as ctx:
         keep = ctx.enter_context(tc.tile_pool(name="keep", bufs=1))
-        ring = ctx.enter_context(tc.tile_pool(name="ring", bufs=3))
+        ring = ctx.enter_context(tc.tile_pool(name="ring", bufs=4))
         psum_h = ctx.enter_context(tc.psum_pool(name="psum_h", bufs=3))
-        psum_y = ctx.enter_context(tc.psum_pool(name="psum_y", bufs=5))
+        psum_t = ctx.enter_context(tc.psum_pool(name="psum_t", bufs=1))
+        psum_y = ctx.enter_context(tc.psum_pool(name="psum_y", bufs=4))
 
         def held(name, shape, dtype):
             return keep.tile(shape, dtype, name=name, align_bytes=64)
 
-        def load_scales(plane, scales, quadrants):
+        def load_scales(plane, scales):
             rows = scales.bitcast(I32)
-            for q in quadrants:
+            for q in range(4):
                 nc.sync.dma_start(
                     out=plane[32 * q : 32 * q + 4, :].rearrange("p (a w) -> p a w", a=PASSES),
                     in_=rows[:, 4 * q : 4 * q + 4, :].rearrange("a r w -> r a w"),
                 )
 
-        def load_words(name, words):
-            tile = held(name, [P, PASSES, words.shape[2]], I32)
-            nc.sync.dma_start(out=tile[:], in_=words.rearrange("a p n i -> p a (n i)").bitcast(I32))
-            return tile
+        wb_codes = {}
+
+        def load_wb(nh):
+            tile = held("wb_codes%d" % nh, [P, PASSES, HALF], I32)
+            words = wb_words.rearrange("a p n i -> p a (n i)").bitcast(I32)
+            nc.sync.dma_start(out=tile[:], in_=words[:, :, nh * HALF : (nh + 1) * HALF])
+            wb_codes[nh] = tile
 
         offsets = keep.tile([P, J // 16], U16, name="offsets")
         tab_plane = held("tab_plane", [P, PASSES * T // 4], I32)
@@ -81,60 +84,40 @@ def tile_list_xcross_none_kernel(
 
         nc.sync.dma_start(offsets[:], offs)
         tab_raw = held("tab_raw", [P, T], I32)
-        dn_raw = {}
-
-        def load_dn(g):
-            tile = held("dn_raw%d" % g, [P, PASSES, PASS], I32)
-            words = dn_words.rearrange("a p n i -> p a (n i)").bitcast(I32)
-            nc.sync.dma_start(out=tile[:], in_=words[:, :, g * PASS : (g + 1) * PASS])
-            dn_raw[g] = tile
-
         nc.sync.dma_start(out=tab_raw[:], in_=tab_words[0].rearrange("p t i -> p (t i)").bitcast(I32))
-        load_scales(tab_plane, tab_scales, (0, 1, 2, 3))
-        load_dn(0)
-        load_scales(dn_plane, dn_scales, (0, 1))
+        load_scales(tab_plane, tab_scales)
+        dn_codes = held("dn_codes", [P, PASSES, R], I32)
+        nc.sync.dma_start(out=dn_codes[:], in_=dn_words.rearrange("a p n i -> p a (n i)").bitcast(I32))
+        load_scales(dn_plane, dn_scales)
         load_up(0, 0)
-        load_scales(dn_plane, dn_scales, (2, 3))
-        load_dn(1)
         load_up(1, 0)
         load_up(0, 1)
-        load_scales(wb_plane, wb_scales, (0, 1, 2, 3))
-        nc.sync.dma_start(out=b_rows[0:NT, :], in_=b.rearrange("(c p) -> c p", p=P))
-        wb_codes = load_words("wb_codes", wb_words)
-        load_x0(0)
-        load_x0(1)
         load_up(1, 1)
-        for c in range(2, NT):
+        load_scales(wb_plane, wb_scales)
+        nc.sync.dma_start(out=b_rows[0:NT, :], in_=b.rearrange("(c p) -> c p", p=P))
+        load_wb(0)
+        for c in range(NT // 2):
+            load_x0(c)
+        load_wb(1)
+        for c in range(NT // 2, NT):
             load_x0(c)
 
         tab_pairs = held("tab_pairs", [P, J], U32)
         tab_codes = held("tab_codes", [P, PASSES, 2 * J], U8)
         tab_sc = held("tab_sc", [P, PASSES, J], U8)
-        dn_codes = [held("dn_codes%d" % g, [P, PASSES, PASS], I32) for g in range(R // PASS)]
-        dn_sc = [held("dn_sc%d" % g, [P, PASSES, PASS], U8) for g in range(R // PASS)]
-        dn_sc_raw = dn_plane[:].bitcast(U8).rearrange("p (a r) -> p a r", a=PASSES)
-
         nc.vector.tensor_copy(tab_pairs[:], tab_raw[:].bitcast(U32).indirect(offsets[:]))
-        nc.vector.tensor_copy(tab_sc[:, 0, :], tab_plane[:].bitcast(U8)[:, 0:T].indirect(offsets[:]))
         nc.vector.tensor_copy(
             out=tab_codes[:].bitcast(U16),
             in_=tab_pairs[:].bitcast(U16).rearrange("p (j a) -> p a j", a=PASSES),
         )
-        nc.vector.tensor_copy(tab_sc[:, 1, :], tab_plane[:].bitcast(U8)[:, T : 2 * T].indirect(offsets[:]))
-
-        def permute_dn(g):
-            cols = slice(g * PASS, (g + 1) * PASS)
-            nc.vector.tensor_copy(
-                out=dn_codes[g][:].rearrange("p a (t m) -> p a m t", t=PACK),
-                in_=dn_raw[g][:].rearrange("p a (m t) -> p a m t", t=PACK),
-            )
-            nc.vector.tensor_copy(
-                out=dn_sc[g][:].rearrange("p a (t m) -> p a m t", t=PACK),
-                in_=dn_sc_raw[:, :, cols].rearrange("p a (m t) -> p a m t", t=PACK),
-            )
-
-        permute_dn(0)
-        permute_dn(1)
+        for jt in range(J // P):
+            picks = offsets[:, jt * P // 16 : (jt + 1) * P // 16]
+            for a in range(PASSES):
+                nc.vector.tensor_copy(
+                    tab_sc[:, a, jt * P : (jt + 1) * P],
+                    tab_plane[:].bitcast(U8)[:, a * T : (a + 1) * T].indirect(picks),
+                )
+        dn_sc = dn_plane[:].bitcast(U8).rearrange("p (a r) -> p a r", a=PASSES)
         wb_sc = wb_plane[:].bitcast(U8).rearrange("p (a n) -> p a n", a=PASSES)
 
         b_ps = psum_y.tile([P, P], F32, name="y_ps")
@@ -171,35 +154,45 @@ def tile_list_xcross_none_kernel(
 
         h_codes = held("h_codes", [P, PASSES, J], U32)
         h_sc = held("h_sc", [P, PASSES, J], U8)
-        h_bf = {}
+        h_pairs = [held("h_pairs%d" % jt, [P, PASSES, P, 2], F32) for jt in range(J // P)]
+        h_rows = {}
 
-        def make_h(g):
-            grouped = held("h_bf%d" % g, [P, J, PACK], BF16)
-            h_bf[g] = grouped
-            for jc in range(J // JC):
-                bank = psum_h.tile([P, PACK, JC], F32, name="h_ps")
-                for t in range(PACK):
-                    cols = slice(t * P, (t + 1) * P)
-                    for a in range(PASSES):
-                        nc.tensor.matmul_mx(
-                            out=bank[:, t, :],
-                            lhsT=dn_codes[g][:, a, cols].bitcast(FP8X4),
-                            lhsT_scale=dn_sc[g][:, a, cols],
-                            rhs=tab_codes[:, a, 2 * jc * JC : 2 * (jc + 1) * JC].bitcast(FP4X4),
-                            rhs_scale=tab_sc[:, a, jc * JC : (jc + 1) * JC],
-                            start=(a == 0),
-                            stop=(a == PASSES - 1),
-                        )
+        def multiply_dn(jt):
+            for g in range(R // PASS):
+                bank = psum_h.tile([P, PASS], F32, name="h_ps")
+                for a in range(PASSES):
+                    nc.tensor.matmul_mx(
+                        out=bank[:],
+                        lhsT=tab_codes[:, a, 2 * jt * P : 2 * (jt + 1) * P].bitcast(FP4X4),
+                        lhsT_scale=tab_sc[:, a, jt * P : (jt + 1) * P],
+                        rhs=dn_codes[:, a, g * PASS : (g + 1) * PASS].bitcast(FP8X4),
+                        rhs_scale=dn_sc[:, a, g * PASS : (g + 1) * PASS],
+                        start=(a == 0),
+                        stop=(a == PASSES - 1),
+                    )
+                rows = held("h_rows%d%d" % (jt, g), [P, PASS], BF16)
                 nc.scalar.copy(
-                    out=grouped[:, jc * JC : (jc + 1) * JC, :], in_=bank[:].rearrange("p t j -> p j t")
+                    out=rows[:].rearrange("j (u p e) -> j u p e", u=2, e=2),
+                    in_=bank[:].rearrange("j (p u e) -> j u p e", u=2, e=2),
                 )
+                h_rows[jt, g] = rows
 
-        def quant_h(g):
-            nc.vector.quantize_mx(
-                out=h_codes[:, g, :].bitcast(FP8X4),
-                scales=h_sc[:, g, :],
-                in_=h_bf[g][:].rearrange("p j t -> p (j t)"),
-            )
+        def turn_h(jt):
+            bank = psum_t.tile([P, PASSES, 2, P], F32, name="t_ps")
+            for g in range(R // PASS):
+                for u in range(2):
+                    nc.tensor.transpose(
+                        bank[:, g, u, :], h_rows[jt, g][:].bitcast(F32)[:, u * P : (u + 1) * P], ident[:]
+                    )
+            nc.scalar.copy(out=h_pairs[jt][:], in_=bank[:].rearrange("p g u j -> p g j u"))
+
+        def quant_h(jt):
+            for g in range(R // PASS):
+                nc.vector.quantize_mx(
+                    out=h_codes[:, g, jt * P : (jt + 1) * P].bitcast(FP8X4),
+                    scales=h_sc[:, g, jt * P : (jt + 1) * P],
+                    in_=h_pairs[jt][:, g, :, :].rearrange("p j u -> p (j u)").bitcast(BF16),
+                )
 
         def make_out(c):
             cols = slice(c * P, (c + 1) * P)
@@ -207,7 +200,7 @@ def tile_list_xcross_none_kernel(
             for a in range(PASSES):
                 nc.tensor.matmul_mx(
                     out=acc[:],
-                    lhsT=wb_codes[:, a, cols].bitcast(FP8X4),
+                    lhsT=wb_codes[c * P // HALF][:, a, c * P % HALF : c * P % HALF + P].bitcast(FP8X4),
                     lhsT_scale=wb_sc[:, a, cols],
                     rhs=tab_codes[:, a, :].bitcast(FP4X4),
                     rhs_scale=tab_sc[:, a, :],
@@ -230,19 +223,23 @@ def tile_list_xcross_none_kernel(
             nc.vector.tensor_tensor(result[:], x0[c][:].indirect(offsets[:]), factor[:], ALU.mult)
             nc.sync.dma_start(out=out[cols, :], in_=result[:])
 
-        make_h(0)
-        make_h(1)
-        round_up(0, 0, False, 4)
+        multiply_dn(0)
+        multiply_dn(1)
+        turn_h(0)
+        multiply_dn(2)
+        turn_h(1)
+        multiply_dn(3)
+        turn_h(2)
+        turn_h(3)
+        round_up(0, 0, True, 1)
         round_up(1, 0, True, 1)
         quant_up(0, 0, 1)
         quant_up(1, 0, 1)
-        quant_h(0)
+        for jt in range(J // P):
+            quant_h(jt)
         round_up(0, 1, True, 1)
-        quant_h(1)
         quant_up(0, 1, 1)
-        for c in range(NT // 2):
-            make_out(c)
-        round_up(1, 1, False, 4)
+        round_up(1, 1, False, 2)
         quant_up(1, 1, 2)
-        for c in range(NT // 2, NT):
+        for c in range(NT):
             make_out(c)

@@ -22,6 +22,7 @@ PACK = 4
 PASS = P * PACK
 PASSES = K // PASS
 NT = N // P
+JT = J // P
 HALF = 512
 
 
@@ -31,29 +32,27 @@ def tile_list_xcross_none_kernel(
     nc = tc.nc
     with ExitStack() as ctx:
         keep = ctx.enter_context(tc.tile_pool(name="keep", bufs=1))
-        ring = ctx.enter_context(tc.tile_pool(name="ring", bufs=4))
-        psum_h = ctx.enter_context(tc.psum_pool(name="psum_h", bufs=3))
-        psum_t = ctx.enter_context(tc.psum_pool(name="psum_t", bufs=1))
-        psum_y = ctx.enter_context(tc.psum_pool(name="psum_y", bufs=4))
+        psum = ctx.enter_context(tc.psum_pool(name="psum", bufs=1))
 
         def held(name, shape, dtype):
             return keep.tile(shape, dtype, name=name, align_bytes=64)
 
-        def load_scales(plane, scales):
+        def in_bank(bank, name, shape):
+            return psum.tile(shape, F32, name=name, tag="bank%d" % bank)
+
+        def load_scales(queue, plane, scales):
             rows = scales.bitcast(I32)
-            for q in range(4):
-                nc.sync.dma_start(
-                    out=plane[32 * q : 32 * q + 4, :].rearrange("p (a w) -> p a w", a=PASSES),
-                    in_=rows[:, 4 * q : 4 * q + 4, :].rearrange("a r w -> r a w"),
+            for r in range(4):
+                queue.dma_start(
+                    out=plane[r:P:32, :].rearrange("p (a w) -> p a w", a=PASSES),
+                    in_=rows[:, r:16:4, :].rearrange("a q w -> q a w"),
                 )
 
-        wb_codes = {}
-
-        def load_wb(nh):
-            tile = held("wb_codes%d" % nh, [P, PASSES, HALF], I32)
-            words = wb_words.rearrange("a p n i -> p a (n i)").bitcast(I32)
-            nc.sync.dma_start(out=tile[:], in_=words[:, :, nh * HALF : (nh + 1) * HALF])
-            wb_codes[nh] = tile
+        def load_word_columns(name, words, half):
+            tile = held("%s%d" % (name, half), [P, PASSES, HALF], I32)
+            view = words.rearrange("a p n i -> p a (n i)").bitcast(I32)
+            nc.sync.dma_start(out=tile[:], in_=view[:, :, half * HALF : (half + 1) * HALF])
+            return tile
 
         offsets = keep.tile([P, J // 16], U16, name="offsets")
         tab_plane = held("tab_plane", [P, PASSES * T // 4], I32)
@@ -69,11 +68,11 @@ def tile_list_xcross_none_kernel(
 
         up_raw = {}
 
-        def load_up(a, nh):
-            raw = held("up_raw%d%d" % (a, nh), [P, PACK, HALF], F32)
-            rows = upw[a * PASS : (a + 1) * PASS, nh * HALF : (nh + 1) * HALF]
+        def load_up(g, nh):
+            raw = held("up_raw%d%d" % (g, nh), [P, PACK, HALF], F32)
+            rows = upw[g * PASS : (g + 1) * PASS, nh * HALF : (nh + 1) * HALF]
             nc.sync.dma_start(out=raw[:], in_=rows.rearrange("(p t) n -> p t n", t=PACK))
-            up_raw[a, nh] = raw
+            up_raw[g, nh] = raw
 
         x0 = {}
 
@@ -82,24 +81,27 @@ def tile_list_xcross_none_kernel(
             nc.sync.dma_start(out=tile[:], in_=x0T[c * P : (c + 1) * P, :])
             x0[c] = tile
 
+        dn_codes = {}
+        wb_codes = {}
+        nc.gpsimd.dma_start(out=b_rows[0:NT, :], in_=b.rearrange("(c p) -> c p", p=P))
         nc.sync.dma_start(offsets[:], offs)
         tab_raw = held("tab_raw", [P, T], I32)
         nc.sync.dma_start(out=tab_raw[:], in_=tab_words[0].rearrange("p t i -> p (t i)").bitcast(I32))
-        load_scales(tab_plane, tab_scales)
-        dn_codes = held("dn_codes", [P, PASSES, R], I32)
-        nc.sync.dma_start(out=dn_codes[:], in_=dn_words.rearrange("a p n i -> p a (n i)").bitcast(I32))
-        load_scales(dn_plane, dn_scales)
+        load_scales(nc.sync, tab_plane, tab_scales)
+        dn_codes[0] = load_word_columns("dn_codes", dn_words, 0)
+        load_scales(nc.sync, dn_plane, dn_scales)
         load_up(0, 0)
+        dn_codes[1] = load_word_columns("dn_codes", dn_words, 1)
+        load_scales(nc.gpsimd, wb_plane, wb_scales)
         load_up(1, 0)
         load_up(0, 1)
+        wb_codes[0] = load_word_columns("wb_codes", wb_words, 0)
+        load_x0(0)
         load_up(1, 1)
-        load_scales(wb_plane, wb_scales)
-        nc.sync.dma_start(out=b_rows[0:NT, :], in_=b.rearrange("(c p) -> c p", p=P))
-        load_wb(0)
-        for c in range(NT // 2):
-            load_x0(c)
-        load_wb(1)
-        for c in range(NT // 2, NT):
+        load_x0(1)
+        load_x0(2)
+        wb_codes[1] = load_word_columns("wb_codes", wb_words, 1)
+        for c in range(3, NT):
             load_x0(c)
 
         tab_pairs = held("tab_pairs", [P, J], U32)
@@ -110,7 +112,7 @@ def tile_list_xcross_none_kernel(
             out=tab_codes[:].bitcast(U16),
             in_=tab_pairs[:].bitcast(U16).rearrange("p (j a) -> p a j", a=PASSES),
         )
-        for jt in range(J // P):
+        for jt in range(JT):
             picks = offsets[:, jt * P // 16 : (jt + 1) * P // 16]
             for a in range(PASSES):
                 nc.vector.tensor_copy(
@@ -120,7 +122,7 @@ def tile_list_xcross_none_kernel(
         dn_sc = dn_plane[:].bitcast(U8).rearrange("p (a r) -> p a r", a=PASSES)
         wb_sc = wb_plane[:].bitcast(U8).rearrange("p (a n) -> p a n", a=PASSES)
 
-        b_ps = psum_y.tile([P, P], F32, name="y_ps")
+        b_ps = in_bank(7, "b_ps", [P, P])
         nc.tensor.transpose(b_ps[:], b_rows[:], ident[:])
         bias1 = held("bias1", [P, NT], F32)
         nc.scalar.activation(out=bias1[:], in_=b_ps[:, 0:NT], func=ACT.Copy, bias=1.0)
@@ -129,117 +131,140 @@ def tile_list_xcross_none_kernel(
         up_sc = held("up_sc", [P, PASSES, N], U8)
         up_bf = {}
 
-        def round_up(a, nh, on_vector, parts):
-            grouped = held("up_bf%d%d" % (a, nh), [P, HALF, PACK], BF16)
-            up_bf[a, nh] = grouped
+        def round_up(g, nh, on_vector, parts):
+            grouped = held("up_bf%d%d" % (g, nh), [P, HALF, PACK], BF16)
+            up_bf[g, nh] = grouped
             width = HALF // parts
             for s in range(parts):
                 cols = slice(s * width, (s + 1) * width)
                 dst = grouped[:, cols, :].rearrange("p (c i) t -> p c t i", i=4)
-                src = up_raw[a, nh][:, :, cols].rearrange("p t (c i) -> p c t i", i=4)
+                src = up_raw[g, nh][:, :, cols].rearrange("p t (c i) -> p c t i", i=4)
                 if on_vector:
                     nc.vector.tensor_copy(out=dst, in_=src)
                 else:
                     nc.scalar.copy(out=dst, in_=src)
 
-        def quant_up(a, nh, parts):
+        def quant_up(g, nh, parts):
             width = HALF // parts
             for s in range(parts):
                 cols = slice(nh * HALF + s * width, nh * HALF + (s + 1) * width)
                 nc.vector.quantize_mx(
-                    out=up_codes[:, a, cols].bitcast(FP8X4),
-                    scales=up_sc[:, a, cols],
-                    in_=up_bf[a, nh][:, s * width : (s + 1) * width, :].rearrange("p n t -> p (n t)"),
+                    out=up_codes[:, g, cols].bitcast(FP8X4),
+                    scales=up_sc[:, g, cols],
+                    in_=up_bf[g, nh][:, s * width : (s + 1) * width, :].rearrange("p n t -> p (n t)"),
                 )
 
         h_codes = held("h_codes", [P, PASSES, J], U32)
         h_sc = held("h_sc", [P, PASSES, J], U8)
-        h_pairs = [held("h_pairs%d" % jt, [P, PASSES, P, 2], F32) for jt in range(J // P)]
         h_rows = {}
+        h_pairs = {}
 
-        def multiply_dn(jt):
-            for g in range(R // PASS):
-                bank = psum_h.tile([P, PASS], F32, name="h_ps")
-                for a in range(PASSES):
-                    nc.tensor.matmul_mx(
-                        out=bank[:],
-                        lhsT=tab_codes[:, a, 2 * jt * P : 2 * (jt + 1) * P].bitcast(FP4X4),
-                        lhsT_scale=tab_sc[:, a, jt * P : (jt + 1) * P],
-                        rhs=dn_codes[:, a, g * PASS : (g + 1) * PASS].bitcast(FP8X4),
-                        rhs_scale=dn_sc[:, a, g * PASS : (g + 1) * PASS],
-                        start=(a == 0),
-                        stop=(a == PASSES - 1),
-                    )
-                rows = held("h_rows%d%d" % (jt, g), [P, PASS], BF16)
-                nc.scalar.copy(
-                    out=rows[:].rearrange("j (u p e) -> j u p e", u=2, e=2),
-                    in_=bank[:].rearrange("j (p u e) -> j u p e", u=2, e=2),
-                )
-                h_rows[jt, g] = rows
-
-        def turn_h(jt):
-            bank = psum_t.tile([P, PASSES, 2, P], F32, name="t_ps")
-            for g in range(R // PASS):
-                for u in range(2):
-                    nc.tensor.transpose(
-                        bank[:, g, u, :], h_rows[jt, g][:].bitcast(F32)[:, u * P : (u + 1) * P], ident[:]
-                    )
-            nc.scalar.copy(out=h_pairs[jt][:], in_=bank[:].rearrange("p g u j -> p g j u"))
-
-        def quant_h(jt):
-            for g in range(R // PASS):
-                nc.vector.quantize_mx(
-                    out=h_codes[:, g, jt * P : (jt + 1) * P].bitcast(FP8X4),
-                    scales=h_sc[:, g, jt * P : (jt + 1) * P],
-                    in_=h_pairs[jt][:, g, :, :].rearrange("p j u -> p (j u)").bitcast(BF16),
-                )
-
-        def make_out(c):
-            cols = slice(c * P, (c + 1) * P)
-            acc = psum_y.tile([P, J], F32, name="y_ps")
+        def multiply_dn(g, jt):
+            acc = in_bank(JT * g + jt, "h_ps", [P, PASS])
             for a in range(PASSES):
                 nc.tensor.matmul_mx(
                     out=acc[:],
-                    lhsT=wb_codes[c * P // HALF][:, a, c * P % HALF : c * P % HALF + P].bitcast(FP8X4),
-                    lhsT_scale=wb_sc[:, a, cols],
-                    rhs=tab_codes[:, a, :].bitcast(FP4X4),
-                    rhs_scale=tab_sc[:, a, :],
+                    lhsT=tab_codes[:, a, 2 * jt * P : 2 * (jt + 1) * P].bitcast(FP4X4),
+                    lhsT_scale=tab_sc[:, a, jt * P : (jt + 1) * P],
+                    rhs=dn_codes[g][:, a, :].bitcast(FP8X4),
+                    rhs_scale=dn_sc[:, a, g * PASS : (g + 1) * PASS],
                     start=(a == 0),
-                    stop=False,
+                    stop=(a == PASSES - 1),
                 )
-            for g in range(PASSES):
-                nc.tensor.matmul_mx(
-                    out=acc[:],
-                    lhsT=up_codes[:, g, cols].bitcast(FP8X4),
-                    lhsT_scale=up_sc[:, g, cols],
-                    rhs=h_codes[:, g, :].bitcast(FP8X4),
-                    rhs_scale=h_sc[:, g, :],
-                    start=False,
-                    stop=(g == PASSES - 1),
-                )
-            factor = ring.tile([P, J], F32, name="factor")
-            nc.scalar.activation(out=factor[:], in_=acc[:], func=ACT.Identity, bias=bias1[:, c : c + 1])
+            rows = held("h_rows%d%d" % (g, jt), [P, PASS], BF16)
+            nc.scalar.copy(
+                out=rows[:].rearrange("j (u p e) -> j u p e", u=2, e=2),
+                in_=acc[:].rearrange("j (p u e) -> j u p e", u=2, e=2),
+            )
+            h_rows[g, jt] = rows
+
+        def turn_h(g, jh):
+            turned = in_bank(JT * g + 2 * jh, "t_ps", [P, 2, 2, P])
+            for s in range(2):
+                for u in range(2):
+                    nc.tensor.transpose(
+                        turned[:, s, u, :],
+                        h_rows[g, 2 * jh + s][:].bitcast(F32)[:, u * P : (u + 1) * P],
+                        ident[:],
+                    )
+            pairs = held("h_pairs%d%d" % (g, jh), [P, 2, P, 2], F32)
+            nc.scalar.copy(out=pairs[:], in_=turned[:].rearrange("p s u j -> p s j u"))
+            h_pairs[g, jh] = pairs
+
+        def quant_h(g, jh):
+            cols = slice(jh * 2 * P, (jh + 1) * 2 * P)
+            nc.vector.quantize_mx(
+                out=h_codes[:, g, cols].bitcast(FP8X4),
+                scales=h_sc[:, g, cols],
+                in_=h_pairs[g, jh][:].rearrange("p s j u -> p (s j u)").bitcast(BF16),
+            )
+
+        y_acc = {}
+
+        def open_y(c):
+            bank = 2 * c + 1 if c < NT // 2 else 2 * (c - NT // 2)
+            y_acc[c] = in_bank(bank, "y_ps", [P, J])
+
+        def wb_pass(c, a, start):
+            nc.tensor.matmul_mx(
+                out=y_acc[c][:],
+                lhsT=wb_codes[c * P // HALF][:, a, c * P % HALF : c * P % HALF + P].bitcast(FP8X4),
+                lhsT_scale=wb_sc[:, a, c * P : (c + 1) * P],
+                rhs=tab_codes[:, a, :].bitcast(FP4X4),
+                rhs_scale=tab_sc[:, a, :],
+                start=start,
+                stop=False,
+            )
+
+        def up_pass(c, g, start):
+            nc.tensor.matmul_mx(
+                out=y_acc[c][:],
+                lhsT=up_codes[:, g, c * P : (c + 1) * P].bitcast(FP8X4),
+                lhsT_scale=up_sc[:, g, c * P : (c + 1) * P],
+                rhs=h_codes[:, g, :].bitcast(FP8X4),
+                rhs_scale=h_sc[:, g, :],
+                start=start,
+                stop=(g == PASSES - 1),
+            )
+
+        def cross(c):
+            factor = held("factor%d" % c, [P, J], F32)
+            nc.scalar.activation(out=factor[:], in_=y_acc[c][:], func=ACT.Identity, bias=bias1[:, c : c + 1])
             result = held("result%d" % c, [P, J], F32)
             nc.vector.tensor_tensor(result[:], x0[c][:].indirect(offsets[:]), factor[:], ALU.mult)
-            nc.sync.dma_start(out=out[cols, :], in_=result[:])
+            nc.sync.dma_start(out=out[c * P : (c + 1) * P, :], in_=result[:])
 
-        multiply_dn(0)
-        multiply_dn(1)
-        turn_h(0)
-        multiply_dn(2)
-        turn_h(1)
-        multiply_dn(3)
-        turn_h(2)
-        turn_h(3)
-        round_up(0, 0, True, 1)
-        round_up(1, 0, True, 1)
-        quant_up(0, 0, 1)
-        quant_up(1, 0, 1)
-        for jt in range(J // P):
-            quant_h(jt)
+        def first_half_tile(c):
+            open_y(c)
+            wb_pass(c, 0, True)
+            wb_pass(c, 1, False)
+            up_pass(c, 0, False)
+            up_pass(c, 1, False)
+            cross(c)
+
+        for g in range(PASSES):
+            for jt in range(JT):
+                multiply_dn(g, jt)
+            for jh in range(2):
+                turn_h(g, jh)
+        for g in range(PASSES):
+            round_up(g, 0, True, 1)
+            quant_up(g, 0, 1)
+            for jh in range(2):
+                quant_h(g, jh)
         round_up(0, 1, True, 1)
         quant_up(0, 1, 1)
+        first_half_tile(0)
+        first_half_tile(1)
         round_up(1, 1, False, 2)
         quant_up(1, 1, 2)
-        for c in range(NT):
-            make_out(c)
+        first_half_tile(2)
+        first_half_tile(3)
+        for c in range(NT // 2, NT):
+            open_y(c)
+            up_pass(c, 0, True)
+        for c in range(NT // 2, NT):
+            wb_pass(c, 0, False)
+            wb_pass(c, 1, False)
+            up_pass(c, 1, False)
+            cross(c)

@@ -83,7 +83,7 @@ def tile_list_xcross_none_kernel(
 
         dn_codes = {}
         wb_codes = {}
-        nc.gpsimd.dma_start(out=b_rows[0:NT, :], in_=b.rearrange("(c p) -> c p", p=P))
+        nc.scalar.dma_start(out=b_rows[0:NT, :], in_=b.rearrange("(c p) -> c p", p=P))
         nc.sync.dma_start(offsets[:], offs)
         tab_raw = held("tab_raw", [P, T], I32)
         nc.sync.dma_start(out=tab_raw[:], in_=tab_words[0].rearrange("p t i -> p (t i)").bitcast(I32))
@@ -92,8 +92,8 @@ def tile_list_xcross_none_kernel(
         load_scales(nc.sync, dn_plane, dn_scales)
         load_up(0, 0)
         dn_codes[1] = load_word_columns("dn_codes", dn_words, 1)
-        load_scales(nc.gpsimd, wb_plane, wb_scales)
         load_up(1, 0)
+        load_scales(nc.sync, wb_plane, wb_scales)
         load_up(0, 1)
         wb_codes[0] = load_word_columns("wb_codes", wb_words, 0)
         load_x0(0)

@@ -62,9 +62,9 @@ def tile_list_xcross_none_kernel(
         nc.vector.memset(dn_plane[:], 0)
         nc.vector.memset(wb_plane[:], 0)
         b_rows = held("b_rows", [P, P], F32)
-        nc.gpsimd.memset(b_rows[:], 0.0)
         ident = held("ident", [P, P], F32)
         make_identity(nc, ident[:])
+        nc.scalar.activation(out=b_rows[:], in_=ident[:], func=ACT.Copy, scale=0.0)
 
         up_raw = {}
 
@@ -81,19 +81,18 @@ def tile_list_xcross_none_kernel(
             nc.sync.dma_start(out=tile[:], in_=x0T[c * P : (c + 1) * P, :])
             x0[c] = tile
 
-        dn_codes = {}
         wb_codes = {}
-        nc.scalar.dma_start(out=b_rows[0:NT, :], in_=b.rearrange("(c p) -> c p", p=P))
         nc.sync.dma_start(offsets[:], offs)
         tab_raw = held("tab_raw", [P, T], I32)
         nc.sync.dma_start(out=tab_raw[:], in_=tab_words[0].rearrange("p t i -> p (t i)").bitcast(I32))
         load_scales(nc.sync, tab_plane, tab_scales)
-        dn_codes[0] = load_word_columns("dn_codes", dn_words, 0)
+        dn_codes = held("dn_codes", [P, PASSES, R], I32)
+        nc.sync.dma_start(out=dn_codes[:], in_=dn_words.rearrange("a p n i -> p a (n i)").bitcast(I32))
         load_scales(nc.sync, dn_plane, dn_scales)
         load_up(0, 0)
-        dn_codes[1] = load_word_columns("dn_codes", dn_words, 1)
         load_up(1, 0)
         load_scales(nc.sync, wb_plane, wb_scales)
+        nc.sync.dma_start(out=b_rows[0:NT, :], in_=b.rearrange("(c p) -> c p", p=P))
         load_up(0, 1)
         wb_codes[0] = load_word_columns("wb_codes", wb_words, 0)
         load_x0(0)
@@ -121,11 +120,6 @@ def tile_list_xcross_none_kernel(
                 )
         dn_sc = dn_plane[:].bitcast(U8).rearrange("p (a r) -> p a r", a=PASSES)
         wb_sc = wb_plane[:].bitcast(U8).rearrange("p (a n) -> p a n", a=PASSES)
-
-        b_ps = in_bank(7, "b_ps", [P, P])
-        nc.tensor.transpose(b_ps[:], b_rows[:], ident[:])
-        bias1 = held("bias1", [P, NT], F32)
-        nc.scalar.activation(out=bias1[:], in_=b_ps[:, 0:NT], func=ACT.Copy, bias=1.0)
 
         up_codes = held("up_codes", [P, PASSES, N], U32)
         up_sc = held("up_sc", [P, PASSES, N], U8)
@@ -166,7 +160,7 @@ def tile_list_xcross_none_kernel(
                     out=acc[:],
                     lhsT=tab_codes[:, a, 2 * jt * P : 2 * (jt + 1) * P].bitcast(FP4X4),
                     lhsT_scale=tab_sc[:, a, jt * P : (jt + 1) * P],
-                    rhs=dn_codes[g][:, a, :].bitcast(FP8X4),
+                    rhs=dn_codes[:, a, g * PASS : (g + 1) * PASS].bitcast(FP8X4),
                     rhs_scale=dn_sc[:, a, g * PASS : (g + 1) * PASS],
                     start=(a == 0),
                     stop=(a == PASSES - 1),
@@ -202,7 +196,7 @@ def tile_list_xcross_none_kernel(
         y_acc = {}
 
         def open_y(c):
-            bank = 2 * c + 1 if c < NT // 2 else 2 * (c - NT // 2)
+            bank = (2 * c + 3) % 8 if c < NT // 2 else 2 * (c - NT // 2)
             y_acc[c] = in_bank(bank, "y_ps", [P, J])
 
         def wb_pass(c, a, start):
@@ -247,6 +241,10 @@ def tile_list_xcross_none_kernel(
                 multiply_dn(g, jt)
             for jh in range(2):
                 turn_h(g, jh)
+        b_ps = in_bank(1, "b_ps", [P, P])
+        nc.tensor.transpose(b_ps[:], b_rows[:], ident[:])
+        bias1 = held("bias1", [P, NT], F32)
+        nc.scalar.activation(out=bias1[:], in_=b_ps[:, 0:NT], func=ACT.Copy, bias=1.0)
         for g in range(PASSES):
             round_up(g, 0, True, 1)
             quant_up(g, 0, 1)

@@ -34,8 +34,8 @@ def tile_list_xcross_none_kernel(
         keep = ctx.enter_context(tc.tile_pool(name="keep", bufs=1))
         psum = ctx.enter_context(tc.psum_pool(name="psum", bufs=1))
 
-        def held(name, shape, dtype):
-            return keep.tile(shape, dtype, name=name, align_bytes=64)
+        def held(name, shape, dtype, bytes_of=None):
+            return keep.tile(shape, dtype, name=name, tag=bytes_of or name, align_bytes=64)
 
         def in_bank(bank, name, shape):
             return psum.tile(shape, F32, name=name, tag="bank%d" % bank)
@@ -94,9 +94,9 @@ def tile_list_xcross_none_kernel(
         load_scales(nc.sync, wb_plane, wb_scales)
         nc.sync.dma_start(out=b_rows[0:NT, :], in_=b.rearrange("(c p) -> c p", p=P))
         load_up(0, 1)
+        load_up(1, 1)
         wb_codes[0] = load_word_columns("wb_codes", wb_words, 0)
         load_x0(0)
-        load_up(1, 1)
         load_x0(1)
         load_x0(2)
         wb_codes[1] = load_word_columns("wb_codes", wb_words, 1)
@@ -122,7 +122,7 @@ def tile_list_xcross_none_kernel(
         wb_sc = wb_plane[:].bitcast(U8).rearrange("p (a n) -> p a n", a=PASSES)
 
         up_codes = held("up_codes", [P, PASSES, N], U32)
-        up_sc = held("up_sc", [P, PASSES, N], U8)
+        up_sc = {}
         up_bf = {}
 
         def round_up(g, nh, on_vector, parts):
@@ -138,18 +138,16 @@ def tile_list_xcross_none_kernel(
                 else:
                     nc.scalar.copy(out=dst, in_=src)
 
-        def quant_up(g, nh, parts):
-            width = HALF // parts
-            for s in range(parts):
-                cols = slice(nh * HALF + s * width, nh * HALF + (s + 1) * width)
-                nc.vector.quantize_mx(
-                    out=up_codes[:, g, cols].bitcast(FP8X4),
-                    scales=up_sc[:, g, cols],
-                    in_=up_bf[g, nh][:, s * width : (s + 1) * width, :].rearrange("p n t -> p (n t)"),
-                )
+        def quant_up(g, nh, bytes_of=None):
+            up_sc[g, nh] = held("up_sc%d%d" % (g, nh), [P, HALF], U8, bytes_of)
+            nc.vector.quantize_mx(
+                out=up_codes[:, g, nh * HALF : (nh + 1) * HALF].bitcast(FP8X4),
+                scales=up_sc[g, nh][:],
+                in_=up_bf[g, nh][:].rearrange("p n t -> p (n t)"),
+            )
 
         h_codes = held("h_codes", [P, PASSES, J], U32)
-        h_sc = held("h_sc", [P, PASSES, J], U8)
+        h_sc = {}
         h_rows = {}
         h_pairs = {}
 
@@ -189,17 +187,16 @@ def tile_list_xcross_none_kernel(
             cols = slice(jh * 2 * P, (jh + 1) * 2 * P)
             nc.vector.quantize_mx(
                 out=h_codes[:, g, cols].bitcast(FP8X4),
-                scales=h_sc[:, g, cols],
+                scales=h_sc[g][:, cols],
                 in_=h_pairs[g, jh][:].rearrange("p s j u -> p (s j u)").bitcast(BF16),
             )
 
         y_acc = {}
 
         def open_y(c):
-            bank = (2 * c + 3) % 8 if c < NT // 2 else 2 * (c - NT // 2)
-            y_acc[c] = in_bank(bank, "y_ps", [P, J])
+            y_acc[c] = in_bank((2 * c + 3) % 8, "y_ps", [P, J])
 
-        def wb_pass(c, a, start):
+        def wb_pass(c, a, start, stop):
             nc.tensor.matmul_mx(
                 out=y_acc[c][:],
                 lhsT=wb_codes[c * P // HALF][:, a, c * P % HALF : c * P % HALF + P].bitcast(FP8X4),
@@ -207,34 +204,40 @@ def tile_list_xcross_none_kernel(
                 rhs=tab_codes[:, a, :].bitcast(FP4X4),
                 rhs_scale=tab_sc[:, a, :],
                 start=start,
-                stop=False,
+                stop=stop,
             )
 
-        def up_pass(c, g, start):
+        def up_pass(c, g, start, stop):
             nc.tensor.matmul_mx(
                 out=y_acc[c][:],
                 lhsT=up_codes[:, g, c * P : (c + 1) * P].bitcast(FP8X4),
-                lhsT_scale=up_sc[:, g, c * P : (c + 1) * P],
+                lhsT_scale=up_sc[g, c * P // HALF][:, c * P % HALF : c * P % HALF + P],
                 rhs=h_codes[:, g, :].bitcast(FP8X4),
-                rhs_scale=h_sc[:, g, :],
+                rhs_scale=h_sc[g][:],
                 start=start,
-                stop=(g == PASSES - 1),
+                stop=stop,
             )
 
-        def cross(c):
-            factor = held("factor%d" % c, [P, J], F32)
+        def cross(c, bytes_of=None):
+            factor = held("factor%d" % c, [P, J], F32, bytes_of)
             nc.scalar.activation(out=factor[:], in_=y_acc[c][:], func=ACT.Identity, bias=bias1[:, c : c + 1])
             result = held("result%d" % c, [P, J], F32)
             nc.vector.tensor_tensor(result[:], x0[c][:].indirect(offsets[:]), factor[:], ALU.mult)
             nc.sync.dma_start(out=out[c * P : (c + 1) * P, :], in_=result[:])
 
-        def first_half_tile(c):
+        def first_half_tile(c, bytes_of=None):
             open_y(c)
-            wb_pass(c, 0, True)
-            wb_pass(c, 1, False)
-            up_pass(c, 0, False)
-            up_pass(c, 1, False)
-            cross(c)
+            if c >= 2:
+                wb_pass(c, 0, True, False)
+                wb_pass(c, 1, False, False)
+                up_pass(c, 0, False, False)
+                up_pass(c, 1, False, True)
+            else:
+                up_pass(c, 0, True, False)
+                up_pass(c, 1, False, False)
+                wb_pass(c, 0, False, False)
+                wb_pass(c, 1, False, True)
+            cross(c, bytes_of)
 
         for g in range(PASSES):
             for jt in range(JT):
@@ -247,22 +250,24 @@ def tile_list_xcross_none_kernel(
         nc.scalar.activation(out=bias1[:], in_=b_ps[:, 0:NT], func=ACT.Copy, bias=1.0)
         for g in range(PASSES):
             round_up(g, 0, True, 1)
-            quant_up(g, 0, 1)
-            for jh in range(2):
-                quant_h(g, jh)
+            quant_up(g, 0)
+        h_sc[0] = held("h_sc0", [P, J], U8, "up_raw10")
+        for jh in range(2):
+            quant_h(0, jh)
         round_up(0, 1, True, 1)
-        quant_up(0, 1, 1)
-        first_half_tile(0)
-        first_half_tile(1)
-        round_up(1, 1, False, 2)
-        quant_up(1, 1, 2)
-        first_half_tile(2)
-        first_half_tile(3)
+        quant_up(0, 1)
+        h_sc[1] = held("h_sc1", [P, J], U8, "up_raw01")
+        for jh in range(2):
+            quant_h(1, jh)
+        round_up(1, 1, True, 1)
+        quant_up(1, 1)
+        for c in range(NT // 2):
+            first_half_tile(c)
         for c in range(NT // 2, NT):
             open_y(c)
-            up_pass(c, 0, True)
+            up_pass(c, 0, True, False)
         for c in range(NT // 2, NT):
-            wb_pass(c, 0, False)
-            wb_pass(c, 1, False)
-            up_pass(c, 1, False)
+            wb_pass(c, 0, False, False)
+            wb_pass(c, 1, False, False)
+            up_pass(c, 1, False, True)
             cross(c)

@@ -133,7 +133,7 @@ def tile_list_xcross_none_kernel(
                 cols = slice(s * width, (s + 1) * width)
                 dst = grouped[:, cols, :].rearrange("p (c i) t -> p c t i", i=4)
                 src = up_raw[g, nh][:, :, cols].rearrange("p t (c i) -> p c t i", i=4)
-                if on_vector:
+                if on_vector[s]:
                     nc.vector.tensor_copy(out=dst, in_=src)
                 else:
                     nc.scalar.copy(out=dst, in_=src)
@@ -223,7 +223,8 @@ def tile_list_xcross_none_kernel(
             nc.scalar.activation(out=factor[:], in_=y_acc[c][:], func=ACT.Identity, bias=bias1[:, c : c + 1])
             result = held("result%d" % c, [P, J], F32)
             nc.vector.tensor_tensor(result[:], x0[c][:].indirect(offsets[:]), factor[:], ALU.mult)
-            nc.sync.dma_start(out=out[c * P : (c + 1) * P, :], in_=result[:])
+            queue = nc.scalar if c % 2 == 1 and c > 1 else nc.sync
+            queue.dma_start(out=out[c * P : (c + 1) * P, :], in_=result[:])
 
         def first_half_tile(c, bytes_of=None):
             open_y(c)
@@ -249,17 +250,17 @@ def tile_list_xcross_none_kernel(
         bias1 = held("bias1", [P, NT], F32)
         nc.scalar.activation(out=bias1[:], in_=b_ps[:, 0:NT], func=ACT.Copy, bias=1.0)
         for g in range(PASSES):
-            round_up(g, 0, True, 1)
+            round_up(g, 0, [True], 1)
             quant_up(g, 0)
         h_sc[0] = held("h_sc0", [P, J], U8, "up_raw10")
         for jh in range(2):
             quant_h(0, jh)
-        round_up(0, 1, True, 1)
+        round_up(0, 1, [True], 1)
         quant_up(0, 1)
         h_sc[1] = held("h_sc1", [P, J], U8, "up_raw01")
         for jh in range(2):
             quant_h(1, jh)
-        round_up(1, 1, True, 1)
+        round_up(1, 1, [True, False], 2)
         quant_up(1, 1)
         for c in range(NT // 2):
             first_half_tile(c)

@@ -35,7 +35,7 @@ def tile_list_xcross_none_kernel(
         psum = ctx.enter_context(tc.psum_pool(name="psum", bufs=1))
 
         def held(name, shape, dtype, bytes_of=None):
-            return keep.tile(shape, dtype, name=name, tag=bytes_of or name, align_bytes=64)
+            return keep.tile(shape, dtype, name=name, tag=bytes_of or name, align_bytes=256)
 
         def in_bank(bank, name, shape):
             return psum.tile(shape, F32, name=name, tag="bank%d" % bank)
@@ -223,8 +223,7 @@ def tile_list_xcross_none_kernel(
             nc.scalar.activation(out=factor[:], in_=y_acc[c][:], func=ACT.Identity, bias=bias1[:, c : c + 1])
             result = held("result%d" % c, [P, J], F32)
             nc.vector.tensor_tensor(result[:], x0[c][:].indirect(offsets[:]), factor[:], ALU.mult)
-            queue = nc.scalar if c % 2 == 1 and c > 1 else nc.sync
-            queue.dma_start(out=out[c * P : (c + 1) * P, :], in_=result[:])
+            nc.sync.dma_start(out=out[c * P : (c + 1) * P, :], in_=result[:])
 
         def first_half_tile(c, bytes_of=None):
             open_y(c)

@@ -24,6 +24,7 @@ PASSES = K // PASS
 NT = N // P
 JT = J // P
 HALF = 512
+STORE_GROUP = [(0, 4)] * 4 + [(4, 2)] * 2 + [(6, 1), (7, 1)]
 
 
 def tile_list_xcross_none_kernel(
@@ -68,11 +69,11 @@ def tile_list_xcross_none_kernel(
 
         up_raw = {}
 
-        def load_up(g, nh):
-            raw = held("up_raw%d%d" % (g, nh), [P, PACK, HALF], F32)
-            rows = upw[g * PASS : (g + 1) * PASS, nh * HALF : (nh + 1) * HALF]
+        def load_up(g):
+            raw = held("up_raw%d" % g, [P, PACK, N], F32)
+            rows = upw[g * PASS : (g + 1) * PASS, :]
             nc.sync.dma_start(out=raw[:], in_=rows.rearrange("(p t) n -> p t n", t=PACK))
-            up_raw[g, nh] = raw
+            up_raw[g] = raw
 
         x0 = {}
 
@@ -82,19 +83,17 @@ def tile_list_xcross_none_kernel(
             x0[c] = tile
 
         wb_codes = {}
-        nc.sync.dma_start(offsets[:], offs)
         tab_raw = held("tab_raw", [P, T], I32)
         nc.sync.dma_start(out=tab_raw[:], in_=tab_words[0].rearrange("p t i -> p (t i)").bitcast(I32))
+        nc.sync.dma_start(offsets[:], offs)
         load_scales(nc.sync, tab_plane, tab_scales)
         dn_codes = held("dn_codes", [P, PASSES, R], I32)
         nc.sync.dma_start(out=dn_codes[:], in_=dn_words.rearrange("a p n i -> p a (n i)").bitcast(I32))
         load_scales(nc.sync, dn_plane, dn_scales)
-        load_up(0, 0)
-        load_up(1, 0)
+        load_up(0)
         load_scales(nc.sync, wb_plane, wb_scales)
         nc.sync.dma_start(out=b_rows[0:NT, :], in_=b.rearrange("(c p) -> c p", p=P))
-        load_up(0, 1)
-        load_up(1, 1)
+        load_up(1)
         wb_codes[0] = load_word_columns("wb_codes", wb_words, 0)
         load_x0(0)
         load_x0(1)
@@ -122,28 +121,23 @@ def tile_list_xcross_none_kernel(
         wb_sc = wb_plane[:].bitcast(U8).rearrange("p (a n) -> p a n", a=PASSES)
 
         up_codes = held("up_codes", [P, PASSES, N], U32)
-        up_sc = {}
+        up_sc = held("up_sc", [P, PASSES, N], U8)
         up_bf = {}
 
-        def round_up(g, nh, on_vector, parts):
-            grouped = held("up_bf%d%d" % (g, nh), [P, HALF, PACK], BF16)
-            up_bf[g, nh] = grouped
-            width = HALF // parts
-            for s in range(parts):
-                cols = slice(s * width, (s + 1) * width)
-                dst = grouped[:, cols, :].rearrange("p (c i) t -> p c t i", i=4)
-                src = up_raw[g, nh][:, :, cols].rearrange("p t (c i) -> p c t i", i=4)
-                if on_vector[s]:
-                    nc.vector.tensor_copy(out=dst, in_=src)
-                else:
-                    nc.scalar.copy(out=dst, in_=src)
+        def round_up(g, first, count, copy):
+            grouped = held("up_bf%d_%d" % (g, first), [P, count * P, PACK], BF16)
+            copy(
+                out=grouped[:].rearrange("p (c i) t -> p c t i", i=4),
+                in_=up_raw[g][:, :, first * P : (first + count) * P].rearrange("p t (c i) -> p c t i", i=4),
+            )
+            up_bf[g, first] = grouped
 
-        def quant_up(g, nh, bytes_of=None):
-            up_sc[g, nh] = held("up_sc%d%d" % (g, nh), [P, HALF], U8, bytes_of)
+        def quant_up(g, first, count):
+            cols = slice(first * P, (first + count) * P)
             nc.vector.quantize_mx(
-                out=up_codes[:, g, nh * HALF : (nh + 1) * HALF].bitcast(FP8X4),
-                scales=up_sc[g, nh][:],
-                in_=up_bf[g, nh][:].rearrange("p n t -> p (n t)"),
+                out=up_codes[:, g, cols].bitcast(FP8X4),
+                scales=up_sc[:, g, cols],
+                in_=up_bf[g, first][:].rearrange("p n t -> p (n t)"),
             )
 
         h_codes = held("h_codes", [P, PASSES, J], U32)
@@ -192,6 +186,7 @@ def tile_list_xcross_none_kernel(
             )
 
         y_acc = {}
+        results = {}
 
         def open_y(c):
             y_acc[c] = in_bank((2 * c + 3) % 8, "y_ps", [P, J])
@@ -211,33 +206,23 @@ def tile_list_xcross_none_kernel(
             nc.tensor.matmul_mx(
                 out=y_acc[c][:],
                 lhsT=up_codes[:, g, c * P : (c + 1) * P].bitcast(FP8X4),
-                lhsT_scale=up_sc[g, c * P // HALF][:, c * P % HALF : c * P % HALF + P],
+                lhsT_scale=up_sc[:, g, c * P : (c + 1) * P],
                 rhs=h_codes[:, g, :].bitcast(FP8X4),
                 rhs_scale=h_sc[g][:],
                 start=start,
                 stop=stop,
             )
 
-        def cross(c, bytes_of=None):
-            factor = held("factor%d" % c, [P, J], F32, bytes_of)
+        def cross(c):
+            factor = held("factor%d" % c, [P, J], F32)
             nc.scalar.activation(out=factor[:], in_=y_acc[c][:], func=ACT.Identity, bias=bias1[:, c : c + 1])
-            result = held("result%d" % c, [P, J], F32)
-            nc.vector.tensor_tensor(result[:], x0[c][:].indirect(offsets[:]), factor[:], ALU.mult)
-            nc.sync.dma_start(out=out[c * P : (c + 1) * P, :], in_=result[:])
-
-        def first_half_tile(c, bytes_of=None):
-            open_y(c)
-            if c >= 2:
-                wb_pass(c, 0, True, False)
-                wb_pass(c, 1, False, False)
-                up_pass(c, 0, False, False)
-                up_pass(c, 1, False, True)
-            else:
-                up_pass(c, 0, True, False)
-                up_pass(c, 1, False, False)
-                wb_pass(c, 0, False, False)
-                wb_pass(c, 1, False, True)
-            cross(c, bytes_of)
+            first, count = STORE_GROUP[c]
+            if c == first:
+                results[first] = held("result%d" % c, [P, count, J], F32)
+            nc.vector.tensor_tensor(results[first][:, c - first, :], x0[c][:].indirect(offsets[:]), factor[:], ALU.mult)
+            if c == first + count - 1:
+                rows = out[first * P : (c + 1) * P, :].rearrange("(e p) j -> p e j", p=P)
+                nc.sync.dma_start(out=rows, in_=results[first][:])
 
         for g in range(PASSES):
             for jt in range(JT):
@@ -249,20 +234,29 @@ def tile_list_xcross_none_kernel(
         bias1 = held("bias1", [P, NT], F32)
         nc.scalar.activation(out=bias1[:], in_=b_ps[:, 0:NT], func=ACT.Copy, bias=1.0)
         for g in range(PASSES):
-            round_up(g, 0, [True], 1)
-            quant_up(g, 0)
-        h_sc[0] = held("h_sc0", [P, J], U8, "up_raw10")
-        for jh in range(2):
-            quant_h(0, jh)
-        round_up(0, 1, [True], 1)
-        quant_up(0, 1)
-        h_sc[1] = held("h_sc1", [P, J], U8, "up_raw01")
-        for jh in range(2):
-            quant_h(1, jh)
-        round_up(1, 1, [True, False], 2)
-        quant_up(1, 1)
+            first = g * NT // 2
+            round_up(0, first, NT // 2, nc.vector.tensor_copy)
+            quant_up(0, first, NT // 2)
+            h_sc[g] = held("h_sc%d" % g, [P, J], U8, "up_bf0_%d" % first)
+            for jh in range(2):
+                quant_h(g, jh)
+        for first in (0, 2):
+            round_up(1, first, 2, nc.vector.tensor_copy)
+            quant_up(1, first, 2)
+        round_up(1, NT // 2, NT // 2, nc.scalar.copy)
+        quant_up(1, NT // 2, NT // 2)
         for c in range(NT // 2):
-            first_half_tile(c)
+            open_y(c)
+            up_pass(c, 0, True, False)
+            if c == 0:
+                wb_pass(c, 0, False, False)
+                wb_pass(c, 1, False, False)
+                up_pass(c, 1, False, True)
+            else:
+                up_pass(c, 1, False, False)
+                wb_pass(c, 0, False, False)
+                wb_pass(c, 1, False, True)
+            cross(c)
         for c in range(NT // 2, NT):
             open_y(c)
             up_pass(c, 0, True, False)

@@ -91,15 +91,14 @@ def tile_list_xcross_none_kernel(
         nc.sync.dma_start(out=dn_codes[:], in_=dn_words.rearrange("a p n i -> p a (n i)").bitcast(I32))
         load_scales(nc.sync, dn_plane, dn_scales)
         load_up(0)
-        load_scales(nc.sync, wb_plane, wb_scales)
         nc.sync.dma_start(out=b_rows[0:NT, :], in_=b.rearrange("(c p) -> c p", p=P))
         load_up(1)
+        load_scales(nc.sync, wb_plane, wb_scales)
         wb_codes[0] = load_word_columns("wb_codes", wb_words, 0)
         load_x0(0)
         load_x0(1)
-        load_x0(2)
         wb_codes[1] = load_word_columns("wb_codes", wb_words, 1)
-        for c in range(3, NT):
+        for c in range(2, NT):
             load_x0(c)
 
         tab_pairs = held("tab_pairs", [P, J], U32)
@@ -185,11 +184,46 @@ def tile_list_xcross_none_kernel(
                 in_=h_pairs[g, jh][:].rearrange("p s j u -> p (s j u)").bitcast(BF16),
             )
 
+        def deal_dn(g):
+            cols = slice(g * PASS, (g + 1) * PASS)
+            words = held("dn_dealt%d" % g, [P, PASSES, PASS], I32)
+            nc.vector.tensor_copy(
+                out=words[:].rearrange("p a (t c i) -> p a c t i", t=PACK, i=4),
+                in_=dn_codes[:, :, cols].rearrange("p a (c i t) -> p a c t i", t=PACK, i=4),
+            )
+            scales = held("dn_sc_dealt%d" % g, [P, PASSES, PASS], U8)
+            nc.vector.tensor_copy(
+                out=scales[:].rearrange("p a (t m) -> p a t m", t=PACK),
+                in_=dn_sc[:, :, cols].rearrange("p a (m t) -> p a t m", t=PACK),
+            )
+            return words, scales
+
+        def multiply_dealt(g, jt, words, scales):
+            acc = in_bank(JT * g + jt, "h_ps", [P, PACK, P])
+            for t in range(PACK):
+                for a in range(PASSES):
+                    nc.tensor.matmul_mx(
+                        out=acc[:, t, :],
+                        lhsT=words[:, a, t * P : (t + 1) * P].bitcast(FP8X4),
+                        lhsT_scale=scales[:, a, t * P : (t + 1) * P],
+                        rhs=tab_codes[:, a, 2 * jt * P : 2 * (jt + 1) * P].bitcast(FP4X4),
+                        rhs_scale=tab_sc[:, a, jt * P : (jt + 1) * P],
+                        start=(a == 0),
+                        stop=(a == PASSES - 1),
+                    )
+            if jt % 2 == 0:
+                h_pairs[g, jt // 2] = held("h_pairs%d%d" % (g, jt // 2), [P, 2, P, 2], F32)
+            grouped = h_pairs[g, jt // 2][:, jt % 2, :, :].rearrange("p j u -> p (j u)").bitcast(BF16)
+            nc.scalar.copy(
+                out=grouped.rearrange("p (j t) -> p j t", t=PACK),
+                in_=acc[:].rearrange("p t j -> p j t"),
+            )
+
         y_acc = {}
         results = {}
 
         def open_y(c):
-            y_acc[c] = in_bank((2 * c + 3) % 8, "y_ps", [P, J])
+            y_acc[c] = in_bank([3, 1, 0, 2, 4, 5, 6, 7][c], "y_ps", [P, J])
 
         def wb_pass(c, a, start, stop):
             nc.tensor.matmul_mx(
@@ -224,44 +258,49 @@ def tile_list_xcross_none_kernel(
                 rows = out[first * P : (c + 1) * P, :].rearrange("(e p) j -> p e j", p=P)
                 nc.sync.dma_start(out=rows, in_=results[first][:])
 
-        for g in range(PASSES):
-            for jt in range(JT):
-                multiply_dn(g, jt)
-            for jh in range(2):
-                turn_h(g, jh)
+        for jt in range(JT):
+            multiply_dn(0, jt)
+        dealt = deal_dn(1)
+        for jh in range(2):
+            multiply_dealt(1, jh, *dealt)
+            turn_h(0, jh)
+        for jt in range(2, JT):
+            multiply_dealt(1, jt, *dealt)
         b_ps = in_bank(1, "b_ps", [P, P])
         nc.tensor.transpose(b_ps[:], b_rows[:], ident[:])
         bias1 = held("bias1", [P, NT], F32)
         nc.scalar.activation(out=bias1[:], in_=b_ps[:, 0:NT], func=ACT.Copy, bias=1.0)
-        for g in range(PASSES):
-            first = g * NT // 2
-            round_up(0, first, NT // 2, nc.vector.tensor_copy)
-            quant_up(0, first, NT // 2)
-            h_sc[g] = held("h_sc%d" % g, [P, J], U8, "up_bf0_%d" % first)
-            for jh in range(2):
-                quant_h(g, jh)
-        for first in (0, 2):
-            round_up(1, first, 2, nc.vector.tensor_copy)
-            quant_up(1, first, 2)
-        round_up(1, NT // 2, NT // 2, nc.scalar.copy)
-        quant_up(1, NT // 2, NT // 2)
-        for c in range(NT // 2):
+        round_up(0, 0, 2, nc.vector.tensor_copy)
+        round_up(0, 2, 2, nc.vector.tensor_copy)
+        quant_up(0, 0, 2)
+        quant_up(0, 2, 2)
+        h_sc[0] = held("h_sc0", [P, J], U8, "up_bf0_0")
+        for jh in range(2):
+            quant_h(0, jh)
+        round_up(0, 4, 2, nc.vector.tensor_copy)
+        round_up(0, 6, 2, nc.vector.tensor_copy)
+        quant_up(0, 4, 2)
+        h_sc[1] = held("h_sc1", [P, J], U8, "up_bf0_4")
+        for jh in range(2):
+            quant_h(1, jh)
+        quant_up(0, 6, 2)
+        round_up(1, 0, 1, nc.vector.tensor_copy)
+        round_up(1, 1, 1, nc.vector.tensor_copy)
+        quant_up(1, 0, 1)
+        round_up(1, 2, 2, nc.vector.tensor_copy)
+        quant_up(1, 1, 1)
+        quant_up(1, 2, 2)
+        round_up(1, 4, 2, nc.scalar.copy)
+        round_up(1, 6, 2, nc.scalar.copy)
+        quant_up(1, 4, 2)
+        quant_up(1, 6, 2)
+        for c in range(NT):
             open_y(c)
             up_pass(c, 0, True, False)
             if c == 0:
-                wb_pass(c, 0, False, False)
-                wb_pass(c, 1, False, False)
-                up_pass(c, 1, False, True)
-            else:
                 up_pass(c, 1, False, False)
-                wb_pass(c, 0, False, False)
-                wb_pass(c, 1, False, True)
-            cross(c)
-        for c in range(NT // 2, NT):
-            open_y(c)
-            up_pass(c, 0, True, False)
-        for c in range(NT // 2, NT):
             wb_pass(c, 0, False, False)
-            wb_pass(c, 1, False, False)
-            up_pass(c, 1, False, True)
+            wb_pass(c, 1, False, c == 0)
+            if c > 0:
+                up_pass(c, 1, False, True)
             cross(c)

@@ -43,10 +43,10 @@ def tile_list_xcross_none_kernel(
 
         def load_scales(queue, plane, scales):
             rows = scales.bitcast(I32)
-            for r in range(4):
+            for quadrant in (0, 2, 1, 3):
                 queue.dma_start(
-                    out=plane[r:P:32, :].rearrange("p (a w) -> p a w", a=PASSES),
-                    in_=rows[:, r:16:4, :].rearrange("a q w -> q a w"),
+                    out=plane[32 * quadrant : 32 * quadrant + 4, :].rearrange("p (a w) -> p a w", a=PASSES),
+                    in_=rows[:, 4 * quadrant : 4 * quadrant + 4, :].rearrange("a q w -> q a w"),
                 )
 
         def load_word_columns(name, words, half):

@@ -24,7 +24,7 @@ PASSES = K // PASS
 NT = N // P
 JT = J // P
 HALF = 512
-STORE_GROUP = [(0, 4)] * 4 + [(4, 2)] * 2 + [(6, 1), (7, 1)]
+STORE_GROUP = [(0, 5)] * 5 + [(5, 2)] * 2 + [(7, 1)]
 
 
 def tile_list_xcross_none_kernel(
@@ -91,7 +91,7 @@ def tile_list_xcross_none_kernel(
         nc.sync.dma_start(out=dn_codes[:], in_=dn_words.rearrange("a p n i -> p a (n i)").bitcast(I32))
         load_scales(nc.sync, dn_plane, dn_scales)
         load_up(0)
-        nc.sync.dma_start(out=b_rows[0:NT, :], in_=b.rearrange("(c p) -> c p", p=P))
+        nc.sync.dma_start(out=b_rows[NT : 2 * NT, :], in_=b.rearrange("(c p) -> c p", p=P))
         load_up(1)
         load_scales(nc.sync, wb_plane, wb_scales)
         wb_codes[0] = load_word_columns("wb_codes", wb_words, 0)
@@ -109,11 +109,11 @@ def tile_list_xcross_none_kernel(
             out=tab_codes[:].bitcast(U16),
             in_=tab_pairs[:].bitcast(U16).rearrange("p (j a) -> p a j", a=PASSES),
         )
-        for jt in range(JT):
-            picks = offsets[:, jt * P // 16 : (jt + 1) * P // 16]
+        for jh in range(2):
+            picks = offsets[:, jh * J // 32 : (jh + 1) * J // 32]
             for a in range(PASSES):
                 nc.vector.tensor_copy(
-                    tab_sc[:, a, jt * P : (jt + 1) * P],
+                    tab_sc[:, a, jh * J // 2 : (jh + 1) * J // 2],
                     tab_plane[:].bitcast(U8)[:, a * T : (a + 1) * T].indirect(picks),
                 )
         dn_sc = dn_plane[:].bitcast(U8).rearrange("p (a r) -> p a r", a=PASSES)
@@ -269,38 +269,36 @@ def tile_list_xcross_none_kernel(
         b_ps = in_bank(1, "b_ps", [P, P])
         nc.tensor.transpose(b_ps[:], b_rows[:], ident[:])
         bias1 = held("bias1", [P, NT], F32)
-        nc.scalar.activation(out=bias1[:], in_=b_ps[:, 0:NT], func=ACT.Copy, bias=1.0)
-        round_up(0, 0, 2, nc.vector.tensor_copy)
-        round_up(0, 2, 2, nc.vector.tensor_copy)
-        quant_up(0, 0, 2)
-        quant_up(0, 2, 2)
+        nc.scalar.activation(out=bias1[:], in_=b_ps[:, NT : 2 * NT], func=ACT.Copy, bias=1.0)
+        round_up(0, 0, 4, nc.vector.tensor_copy)
+        round_up(0, 4, 4, nc.vector.tensor_copy)
+        quant_up(0, 0, 4)
         h_sc[0] = held("h_sc0", [P, J], U8, "up_bf0_0")
         for jh in range(2):
             quant_h(0, jh)
-        round_up(0, 4, 2, nc.vector.tensor_copy)
-        round_up(0, 6, 2, nc.vector.tensor_copy)
-        quant_up(0, 4, 2)
+        quant_up(0, 4, 4)
         h_sc[1] = held("h_sc1", [P, J], U8, "up_bf0_4")
         for jh in range(2):
             quant_h(1, jh)
-        quant_up(0, 6, 2)
-        round_up(1, 0, 1, nc.vector.tensor_copy)
-        round_up(1, 1, 1, nc.vector.tensor_copy)
-        quant_up(1, 0, 1)
+        round_up(1, 0, 2, nc.vector.tensor_copy)
         round_up(1, 2, 2, nc.vector.tensor_copy)
-        quant_up(1, 1, 1)
+        quant_up(1, 0, 2)
         quant_up(1, 2, 2)
-        round_up(1, 4, 2, nc.scalar.copy)
-        round_up(1, 6, 2, nc.scalar.copy)
-        quant_up(1, 4, 2)
-        quant_up(1, 6, 2)
+        round_up(1, 4, 4, nc.scalar.copy)
+        quant_up(1, 4, 4)
         for c in range(NT):
             open_y(c)
-            up_pass(c, 0, True, False)
-            if c == 0:
-                up_pass(c, 1, False, False)
-            wb_pass(c, 0, False, False)
-            wb_pass(c, 1, False, c == 0)
-            if c > 0:
+            if c < NT // 2:
+                up_pass(c, 0, True, False)
+                if c == 0:
+                    up_pass(c, 1, False, False)
+                wb_pass(c, 0, False, False)
+                wb_pass(c, 1, False, c == 0)
+                if c > 0:
+                    up_pass(c, 1, False, True)
+            else:
+                wb_pass(c, 0, True, False)
+                wb_pass(c, 1, False, False)
+                up_pass(c, 0, False, False)
                 up_pass(c, 1, False, True)
             cross(c)

from contextlib import ExitStack

import concourse.mybir as mybir
from concourse.masks import make_identity

K, R, N, T, J = 1024, 1024, 1024, 1024, 512
FLOPS = 2 * J * (K * R + K * N + R * N)

F32 = mybir.dt.float32
BF16 = mybir.dt.bfloat16
I32 = mybir.dt.int32
U32 = mybir.dt.uint32
U16 = mybir.dt.uint16
U8 = mybir.dt.uint8
FP8X4 = mybir.dt.float8_e4m3fn_x4
FP4X4 = mybir.dt.float4_e2m1fn_x4
ACT = mybir.ActivationFunctionType
ALU = mybir.AluOpType

P = 128
PACK = 4
PASS = P * PACK
PASSES = K // PASS
NT = N // P
JT = J // P
HALF = 512
STORE_GROUP = [(0, 5)] * 5 + [(5, 2)] * 2 + [(7, 1)]


def tile_list_xcross_none_kernel(
    tc, tab_words, tab_scales, wb_words, wb_scales, dn_words, dn_scales, upw, x0T, b, offs, out
):
    nc = tc.nc
    with ExitStack() as ctx:
        keep = ctx.enter_context(tc.tile_pool(name="keep", bufs=1))
        psum = ctx.enter_context(tc.psum_pool(name="psum", bufs=1))

        def held(name, shape, dtype, bytes_of=None):
            return keep.tile(shape, dtype, name=name, tag=bytes_of or name, align_bytes=256)

        def in_bank(bank, name, shape):
            return psum.tile(shape, F32, name=name, tag="bank%d" % bank)

        def load_scales(queue, plane, scales):
            rows = scales.bitcast(I32)
            for quadrant in (0, 2, 1, 3):
                queue.dma_start(
                    out=plane[32 * quadrant : 32 * quadrant + 4, :].rearrange("p (a w) -> p a w", a=PASSES),
                    in_=rows[:, 4 * quadrant : 4 * quadrant + 4, :].rearrange("a q w -> q a w"),
                )

        def load_word_columns(name, words, half):
            tile = held("%s%d" % (name, half), [P, PASSES, HALF], I32)
            view = words.rearrange("a p n i -> p a (n i)").bitcast(I32)
            nc.sync.dma_start(out=tile[:], in_=view[:, :, half * HALF : (half + 1) * HALF])
            return tile

        offsets = keep.tile([P, J // 16], U16, name="offsets")
        tab_plane = held("tab_plane", [P, PASSES * T // 4], I32)
        dn_plane = held("dn_plane", [P, PASSES * R // 4], I32)
        wb_plane = held("wb_plane", [P, PASSES * N // 4], I32)
        nc.gpsimd.memset(tab_plane[:], 0)
        nc.vector.memset(dn_plane[:], 0)
        nc.vector.memset(wb_plane[:], 0)
        b_rows = held("b_rows", [P, P], F32)
        ident = held("ident", [P, P], F32)
        make_identity(nc, ident[:])
        nc.scalar.activation(out=b_rows[:], in_=ident[:], func=ACT.Copy, scale=0.0)

        up_raw = {}

        def load_up(g):
            raw = held("up_raw%d" % g, [P, PACK, N], F32)
            rows = upw[g * PASS : (g + 1) * PASS, :]
            nc.sync.dma_start(out=raw[:], in_=rows.rearrange("(p t) n -> p t n", t=PACK))
            up_raw[g] = raw

        x0 = {}

        def load_x0(c):
            tile = held("x0_%d" % c, [P, T], F32)
            nc.sync.dma_start(out=tile[:], in_=x0T[c * P : (c + 1) * P, :])
            x0[c] = tile

        wb_codes = {}
        tab_raw = held("tab_raw", [P, T], I32)
        nc.sync.dma_start(out=tab_raw[:], in_=tab_words[0].rearrange("p t i -> p (t i)").bitcast(I32))
        nc.sync.dma_start(offsets[:], offs)
        load_scales(nc.sync, tab_plane, tab_scales)
        dn_codes = held("dn_codes", [P, PASSES, R], I32)
        nc.sync.dma_start(out=dn_codes[:], in_=dn_words.rearrange("a p n i -> p a (n i)").bitcast(I32))
        load_scales(nc.sync, dn_plane, dn_scales)
        load_up(0)
        nc.sync.dma_start(out=b_rows[NT : 2 * NT, :], in_=b.rearrange("(c p) -> c p", p=P))
        load_up(1)
        load_scales(nc.sync, wb_plane, wb_scales)
        wb_codes[0] = load_word_columns("wb_codes", wb_words, 0)
        load_x0(0)
        load_x0(1)
        wb_codes[1] = load_word_columns("wb_codes", wb_words, 1)
        for c in range(2, NT):
            load_x0(c)

        tab_pairs = held("tab_pairs", [P, J], U32)
        tab_codes = held("tab_codes", [P, PASSES, 2 * J], U8)
        tab_sc = held("tab_sc", [P, PASSES, J], U8)
        nc.vector.tensor_copy(tab_pairs[:], tab_raw[:].bitcast(U32).indirect(offsets[:]))
        nc.vector.tensor_copy(
            out=tab_codes[:].bitcast(U16),
            in_=tab_pairs[:].bitcast(U16).rearrange("p (j a) -> p a j", a=PASSES),
        )
        for jh in range(2):
            picks = offsets[:, jh * J // 32 : (jh + 1) * J // 32]
            for a in range(PASSES):
                nc.vector.tensor_copy(
                    tab_sc[:, a, jh * J // 2 : (jh + 1) * J // 2],
                    tab_plane[:].bitcast(U8)[:, a * T : (a + 1) * T].indirect(picks),
                )
        dn_sc = dn_plane[:].bitcast(U8).rearrange("p (a r) -> p a r", a=PASSES)
        wb_sc = wb_plane[:].bitcast(U8).rearrange("p (a n) -> p a n", a=PASSES)

        up_codes = held("up_codes", [P, PASSES, N], U32)
        up_sc = held("up_sc", [P, PASSES, N], U8)
        up_bf = {}

        def round_up(g, first, count, copy):
            grouped = held("up_bf%d_%d" % (g, first), [P, count * P, PACK], BF16)
            copy(
                out=grouped[:].rearrange("p (c i) t -> p c t i", i=4),
                in_=up_raw[g][:, :, first * P : (first + count) * P].rearrange("p t (c i) -> p c t i", i=4),
            )
            up_bf[g, first] = grouped

        def quant_up(g, first, count):
            cols = slice(first * P, (first + count) * P)
            nc.vector.quantize_mx(
                out=up_codes[:, g, cols].bitcast(FP8X4),
                scales=up_sc[:, g, cols],
                in_=up_bf[g, first][:].rearrange("p n t -> p (n t)"),
            )

        h_codes = held("h_codes", [P, PASSES, J], U32)
        h_sc = {}
        h_rows = {}
        h_pairs = {}

        def multiply_dn(g, jt):
            acc = in_bank(JT * g + jt, "h_ps", [P, PASS])
            for a in range(PASSES):
                nc.tensor.matmul_mx(
                    out=acc[:],
                    lhsT=tab_codes[:, a, 2 * jt * P : 2 * (jt + 1) * P].bitcast(FP4X4),
                    lhsT_scale=tab_sc[:, a, jt * P : (jt + 1) * P],
                    rhs=dn_codes[:, a, g * PASS : (g + 1) * PASS].bitcast(FP8X4),
                    rhs_scale=dn_sc[:, a, g * PASS : (g + 1) * PASS],
                    start=(a == 0),
                    stop=(a == PASSES - 1),
                )
            rows = held("h_rows%d%d" % (g, jt), [P, PASS], BF16)
            nc.scalar.copy(
                out=rows[:].rearrange("j (u p e) -> j u p e", u=2, e=2),
                in_=acc[:].rearrange("j (p u e) -> j u p e", u=2, e=2),
            )
            h_rows[g, jt] = rows

        def turn_h(g, jh):
            turned = in_bank(JT * g + 2 * jh, "t_ps", [P, 2, 2, P])
            for s in range(2):
                for u in range(2):
                    nc.tensor.transpose(
                        turned[:, s, u, :],
                        h_rows[g, 2 * jh + s][:].bitcast(F32)[:, u * P : (u + 1) * P],
                        ident[:],
                    )
            pairs = held("h_pairs%d%d" % (g, jh), [P, 2, P, 2], F32)
            nc.scalar.copy(out=pairs[:], in_=turned[:].rearrange("p s u j -> p s j u"))
            h_pairs[g, jh] = pairs

        def quant_h(g, jh):
            cols = slice(jh * 2 * P, (jh + 1) * 2 * P)
            nc.vector.quantize_mx(
                out=h_codes[:, g, cols].bitcast(FP8X4),
                scales=h_sc[g][:, cols],
                in_=h_pairs[g, jh][:].rearrange("p s j u -> p (s j u)").bitcast(BF16),
            )

        def deal_dn(g):
            cols = slice(g * PASS, (g + 1) * PASS)
            words = held("dn_dealt%d" % g, [P, PASSES, PASS], I32)
            nc.vector.tensor_copy(
                out=words[:].rearrange("p a (t c i) -> p a c t i", t=PACK, i=4),
                in_=dn_codes[:, :, cols].rearrange("p a (c i t) -> p a c t i", t=PACK, i=4),
            )
            scales = held("dn_sc_dealt%d" % g, [P, PASSES, PASS], U8)
            nc.vector.tensor_copy(
                out=scales[:].rearrange("p a (t m) -> p a t m", t=PACK),
                in_=dn_sc[:, :, cols].rearrange("p a (m t) -> p a t m", t=PACK),
            )
            return words, scales

        def multiply_dealt(g, jt, words, scales):
            acc = in_bank(JT * g + jt, "h_ps", [P, PACK, P])
            for t in range(PACK):
                for a in range(PASSES):
                    nc.tensor.matmul_mx(
                        out=acc[:, t, :],
                        lhsT=words[:, a, t * P : (t + 1) * P].bitcast(FP8X4),
                        lhsT_scale=scales[:, a, t * P : (t + 1) * P],
                        rhs=tab_codes[:, a, 2 * jt * P : 2 * (jt + 1) * P].bitcast(FP4X4),
                        rhs_scale=tab_sc[:, a, jt * P : (jt + 1) * P],
                        start=(a == 0),
                        stop=(a == PASSES - 1),
                    )
            if jt % 2 == 0:
                h_pairs[g, jt // 2] = held("h_pairs%d%d" % (g, jt // 2), [P, 2, P, 2], F32)
            grouped = h_pairs[g, jt // 2][:, jt % 2, :, :].rearrange("p j u -> p (j u)").bitcast(BF16)
            nc.scalar.copy(
                out=grouped.rearrange("p (j t) -> p j t", t=PACK),
                in_=acc[:].rearrange("p t j -> p j t"),
            )

        y_acc = {}
        results = {}

        def open_y(c):
            y_acc[c] = in_bank([3, 1, 0, 2, 4, 5, 6, 7][c], "y_ps", [P, J])

        def wb_pass(c, a, start, stop):
            nc.tensor.matmul_mx(
                out=y_acc[c][:],
                lhsT=wb_codes[c * P // HALF][:, a, c * P % HALF : c * P % HALF + P].bitcast(FP8X4),
                lhsT_scale=wb_sc[:, a, c * P : (c + 1) * P],
                rhs=tab_codes[:, a, :].bitcast(FP4X4),
                rhs_scale=tab_sc[:, a, :],
                start=start,
                stop=stop,
            )

        def up_pass(c, g, start, stop):
            nc.tensor.matmul_mx(
                out=y_acc[c][:],
                lhsT=up_codes[:, g, c * P : (c + 1) * P].bitcast(FP8X4),
                lhsT_scale=up_sc[:, g, c * P : (c + 1) * P],
                rhs=h_codes[:, g, :].bitcast(FP8X4),
                rhs_scale=h_sc[g][:],
                start=start,
                stop=stop,
            )

        def cross(c):
            factor = held("factor%d" % c, [P, J], F32)
            nc.scalar.activation(out=factor[:], in_=y_acc[c][:], func=ACT.Identity, bias=bias1[:, c : c + 1])
            first, count = STORE_GROUP[c]
            if c == first:
                results[first] = held("result%d" % c, [P, count, J], F32)
            nc.vector.tensor_tensor(results[first][:, c - first, :], x0[c][:].indirect(offsets[:]), factor[:], ALU.mult)
            if c == first + count - 1:
                rows = out[first * P : (c + 1) * P, :].rearrange("(e p) j -> p e j", p=P)
                nc.sync.dma_start(out=rows, in_=results[first][:])

        for jt in range(JT):
            multiply_dn(0, jt)
        dealt = deal_dn(1)
        for jh in range(2):
            multiply_dealt(1, jh, *dealt)
            turn_h(0, jh)
        for jt in range(2, JT):
            multiply_dealt(1, jt, *dealt)
        b_ps = in_bank(1, "b_ps", [P, P])
        nc.tensor.transpose(b_ps[:], b_rows[:], ident[:])
        bias1 = held("bias1", [P, NT], F32)
        nc.scalar.activation(out=bias1[:], in_=b_ps[:, NT : 2 * NT], func=ACT.Copy, bias=1.0)
        round_up(0, 0, 4, nc.vector.tensor_copy)
        round_up(0, 4, 4, nc.vector.tensor_copy)
        quant_up(0, 0, 4)
        h_sc[0] = held("h_sc0", [P, J], U8, "up_bf0_0")
        for jh in range(2):
            quant_h(0, jh)
        quant_up(0, 4, 4)
        h_sc[1] = held("h_sc1", [P, J], U8, "up_bf0_4")
        for jh in range(2):
            quant_h(1, jh)
        round_up(1, 0, 2, nc.vector.tensor_copy)
        round_up(1, 2, 2, nc.vector.tensor_copy)
        quant_up(1, 0, 2)
        quant_up(1, 2, 2)
        round_up(1, 4, 4, nc.scalar.copy)
        quant_up(1, 4, 4)
        for c in range(NT):
            open_y(c)
            if c < NT // 2:
                up_pass(c, 0, True, False)
                if c == 0:
                    up_pass(c, 1, False, False)
                wb_pass(c, 0, False, False)
                wb_pass(c, 1, False, c == 0)
                if c > 0:
                    up_pass(c, 1, False, True)
            else:
                wb_pass(c, 0, True, False)
                wb_pass(c, 1, False, False)
                up_pass(c, 0, False, False)
                up_pass(c, 1, False, True)
            cross(c)
